import numpy as np
import ml_dtypes


def mxq(x, axis, fmt="e4m3"):
    dtype, down = {"e4m3": (ml_dtypes.float8_e4m3fn, 7), "e5m2": (ml_dtypes.float8_e5m2, 14)}[fmt]
    v = np.moveaxis(np.asarray(x, np.float32).astype(ml_dtypes.bfloat16).astype(np.float64), axis, -1)
    blocks = v.reshape(v.shape[:-1] + (-1, 32))
    amax = np.abs(blocks).max(-1, keepdims=True)
    byte = np.maximum(np.where(amax > 0, np.frexp(amax)[1] - 1 + 127, 0) - down, 1)
    scale = np.exp2(byte - 127.0)
    codes = (blocks / scale).astype(np.float32).astype(dtype).astype(np.float64)
    return np.moveaxis((codes * scale).reshape(v.shape), -1, axis)


WIDE = False


def mx_kscale(k):
    if not WIDE:
        return np.ones(k)
    levels = np.array([30, -30])
    if k % 512:
        return np.exp2(np.random.permutation(np.resize(levels, k // 32))).repeat(32)
    a = np.empty((k // 512, 16))
    for p in range(k // 512):
        a[p, :8] = np.random.permutation(np.resize(levels, 8))
        for g in range(8):
            far = levels[np.abs(levels - a[p, g]) >= 10]
            a[p, g + 8] = far[np.random.randint(len(far))]
    return np.exp2(a.ravel()).repeat(32)


def f64(x):
    return np.asarray(x).astype(np.float64)


def striped(idx):
    return np.tile(np.asarray(idx).reshape(-1, 16).T, (8, 1)).astype(np.uint16)


def unstriped(offs):
    return offs[:16].T.reshape(-1).astype(np.int64)


E2M1 = np.array([0.0, 0.5, 1.0, 1.5, 2.0, 3.0, 4.0, 6.0, -0.0, -0.5, -1.0, -1.5, -2.0, -3.0, -4.0, -6.0])


def pack_weight(w, fmt):
    k, n = w.shape
    w = f64(np.asarray(w, np.float32).astype(ml_dtypes.bfloat16)).reshape(k // 32, 32, n)
    amax = np.abs(w).max(1)
    if fmt in ("e4m3", "e5m2"):
        byte = np.frexp(amax)[1] - 1 + 127 - (7 if fmt == "e4m3" else 14)
    else:
        mant, ex = np.frexp(amax / 6.0)
        byte = np.where(mant > 0.5, ex, ex - 1) + 127
    byte = np.clip(np.where(amax > 0, byte, 1), 1, 254)
    scaled = (w * np.exp2(127.0 - byte)[:, None, :]).reshape(k, n).astype(np.float32)
    by_word = np.ascontiguousarray(scaled.reshape(k // 512, 128, 4, n).transpose(0, 1, 3, 2))
    if fmt in ("e4m3", "e5m2"):
        words = by_word.astype(ml_dtypes.float8_e4m3fn if fmt == "e4m3" else ml_dtypes.float8_e5m2).view(np.uint8)
    else:
        c = by_word.astype(ml_dtypes.float4_e2m1fn).view(np.uint8) & 0xF
        words = (c[..., 0::2] | (c[..., 1::2] << 4)).reshape(k // 512, 128, 2 * n)
    return np.ascontiguousarray(words), np.ascontiguousarray(byte.astype(np.uint8).reshape(k // 512, 16, n))


def unpack_weight(words, scales, fmt):
    g, _, n = scales.shape
    words = np.ascontiguousarray(words).reshape(g, 128, n, -1)
    if fmt in ("e4m3", "e5m2"):
        vals = words.view(ml_dtypes.float8_e4m3fn if fmt == "e4m3" else ml_dtypes.float8_e5m2).astype(np.float64)
    else:
        nib = np.empty((g, 128, n, 4), np.uint8)
        nib[..., 0::2] = words & 0xF
        nib[..., 1::2] = words >> 4
        vals = E2M1[nib]
    vals = vals * np.repeat(np.exp2(scales.astype(np.float64) - 127.0), 8, axis=1)[..., None]
    return vals.transpose(0, 1, 3, 2).reshape(g * 512, n)


K, T, J, R, F, N = 512, 512, 256, 512, 512, 256


def setup_inputs():
    n = np.random.standard_normal
    idx = np.random.permutation(T)[:J]
    idx2 = np.random.permutation(T)[:J]
    fk = mx_kscale(K)
    fr = mx_kscale(R)
    ff = mx_kscale(F)
    wp = pack_weight(n((K, R)) * 1 / np.sqrt(K) * fk[:, None] * fr, "e4m3")
    sxp = pack_weight(n((F, J)) / ff[:, None], "e2m1")
    w2p = pack_weight(n((F, R)) * 1 / np.sqrt(F) * ff[:, None] * fr, "e5m2")
    wbp = pack_weight(n((R, N)) * 1 / np.sqrt(R) / fr[:, None], "e2m1")
    return {
        "xf": (n((K, T))).astype(np.float32),
        "fk": (np.random.uniform(0.5, 2.0, (K, 1)) / fk[:, None]).astype(np.float32),
        "w_words": wp[0],
        "w_scales": wp[1],
        "sx_words": sxp[0],
        "sx_scales": sxp[1],
        "w2_words": w2p[0],
        "w2_scales": w2p[1],
        "wb_words": wbp[0],
        "wb_scales": wbp[1],
        "rs": (1.0 * n((J, N))).astype(np.float32),
        "offs": striped(idx),
        "offs2": striped(idx2),
    }


def reference(xf, fk, w_words, w_scales, sx_words, sx_scales, w2_words, w2_scales, wb_words, wb_scales, rs, offs, offs2):
    idx = unstriped(offs)
    idx2 = unstriped(offs2)
    wu = unpack_weight(w_words, w_scales, "e4m3")
    sxu = unpack_weight(sx_words, sx_scales, "e2m1")
    w2u = unpack_weight(w2_words, w2_scales, "e5m2")
    wbu = unpack_weight(wb_words, wb_scales, "e2m1")
    u = np.maximum(f64(xf)[:, idx], f64(xf)[:, idx2]) * f64(fk)
    uq = mxq(u, 0, "e4m3")
    a = wu.T @ uq + w2u.T @ sxu
    ha = np.maximum(a, 0.0)
    h1 = np.pad(ha, ((0, 0), (2, 0)))[:, :J]
    hid = ha - 0.5 * h1
    hidq = mxq(hid, 0, "e5m2")
    p = hidq.T @ wbu
    mn = np.mean(np.abs(p), axis=1, keepdims=True)
    y = np.maximum(p - mn, 0.0) - 0.3 * f64(rs)
    return y

@@ -1,0 +1,214 @@
+from contextlib import ExitStack
+
+import concourse.mybir as mybir
+
+K, T, J, R, F, N = 512, 512, 256, 512, 512, 256
+FLOPS = 2 * (K * R * J + F * R * J + R * J * N)
+
+F32 = mybir.dt.float32
+BF16 = mybir.dt.bfloat16
+I32 = mybir.dt.int32
+U32 = mybir.dt.uint32
+U16 = mybir.dt.uint16
+U8 = mybir.dt.uint8
+E4M3 = mybir.dt.float8_e4m3fn_x4
+E5M2 = mybir.dt.float8_e5m2_x4
+E2M1 = mybir.dt.float4_e2m1fn_x4
+ALU = mybir.AluOpType
+ACT = mybir.ActivationFunctionType
+
+P = 128
+PACK = 4
+HALF = 128
+LAG = 2
+W_ROW = 4
+
+
+def tile_list_sum_largerpicks_own_lagged_rowabove_kernel(
+    tc, xf, fk, w_words, w_scales, sx_words, sx_scales, w2_words, w2_scales, wb_words, wb_scales, rs, offs, offs2, out
+):
+    nc = tc.nc
+    halves = J // HALF
+    cols = HALF // 16
+    with ExitStack() as ctx:
+        sb = ctx.enter_context(tc.tile_pool(name="sb", bufs=1))
+        ps = ctx.enter_context(tc.psum_pool(name="ps", bufs=1))
+
+        list_a = sb.tile([P, J // 16], U16, name="list_a")
+        list_b = sb.tile([P, J // 16], U16, name="list_b")
+        x0 = sb.tile([P, T], F32, name="x0")
+        x1 = sb.tile([P, T], F32, name="x1")
+        x23 = sb.tile([P, 2, T], F32, name="x23")
+        windows = [x0[:], x1[:], x23[:, 0, :], x23[:, 1, :]]
+        factor = sb.tile([P, PACK], F32, name="factor")
+        w_raw = sb.tile([P, R], U32, name="w_raw")
+        w2_raw = sb.tile([P, R], U32, name="w2_raw")
+        ws_raw = sb.tile([P, R], U8, name="ws_raw")
+        w_codes = sb.tile([P, R], U32, name="w_codes", align_bytes=64)
+        w2_codes = sb.tile([P, R], U32, name="w2_codes", align_bytes=64)
+        ws = sb.tile([P, R], U8, name="ws", align_bytes=64)
+        sx_codes = sb.tile([P, 2 * J], U8, name="sx_codes", align_bytes=64)
+        sx_s = sb.tile([P, J], U8, name="sx_s", align_bytes=64)
+        wb_codes = sb.tile([P, 2 * N], U8, name="wb_codes", align_bytes=64)
+        wb_s = sb.tile([P, N], U8, name="wb_s", align_bytes=64)
+        resid = sb.tile([P, halves, N], F32, name="resid")
+        ha = sb.tile([P, (J + LAG) * PACK], F32, name="ha")
+
+        def load_scale_row(queue, tile, first, scales, r):
+            queue.dma_start(out=tile[:].bitcast(I32)[first + r : P : 32, :], in_=scales[0, r:16:4, :].bitcast(I32))
+
+        nc.vector.memset(ws_raw[:].bitcast(U32), 0)
+        nc.gpsimd.memset(sx_s[:].bitcast(U32), 0)
+        nc.vector.memset(wb_s[:].bitcast(U32), 0)
+        nc.vector.memset(ha[:, 0 : LAG * PACK], 0.0)
+
+        planes = xf.rearrange("(p i) t -> p i t", i=PACK)
+        nc.sync.dma_start(list_a[:], offs)
+        nc.sync.dma_start(list_b[:], offs2)
+        nc.sync.dma_start(out=x0[:], in_=planes[:, 0, :])
+        nc.sync.dma_start(out=x1[:], in_=planes[:, 1, :])
+        for r in range(3):
+            load_scale_row(nc.sync, ws_raw, 0, w2_scales, r)
+        nc.sync.dma_start(out=x23[:], in_=planes[:, 2:4, :])
+        load_scale_row(nc.sync, ws_raw, 0, w2_scales, 3)
+        for r in range(4):
+            load_scale_row(nc.sync, ws_raw, W_ROW, w_scales, r)
+        nc.sync.dma_start(out=w2_raw[:].bitcast(I32), in_=w2_words[0].rearrange("p n t -> p (n t)").bitcast(I32))
+        nc.sync.dma_start(out=w_raw[:].bitcast(I32), in_=w_words[0].rearrange("p n t -> p (n t)").bitcast(I32))
+        nc.sync.dma_start(out=sx_codes[:].bitcast(I32), in_=sx_words[0].bitcast(I32))
+        nc.sync.dma_start(out=wb_codes[:].bitcast(I32), in_=wb_words[0].bitcast(I32))
+        for r in range(4):
+            load_scale_row(nc.sync, wb_s, 0, wb_scales, r)
+        nc.sync.dma_start(out=resid[:], in_=rs.rearrange("(h p) n -> p h n", p=P))
+        nc.gpsimd.dma_start(out=factor[:], in_=fk.rearrange("(p i) o -> p (i o)", i=PACK))
+        for r in range(4):
+            load_scale_row(nc.gpsimd, sx_s, 0, sx_scales, r)
+
+        ga = [sb.tile([P, PACK, HALF], F32, name=f"ga{h}") for h in range(halves)]
+        gb = [sb.tile([P, PACK, HALF], F32, name=f"gb{h}") for h in range(halves)]
+        big = [sb.tile([P, PACK, HALF], F32, name=f"big{h}") for h in range(halves)]
+        u = [sb.tile([P, HALF * PACK], BF16, name=f"u{h}", align_bytes=64) for h in range(halves)]
+        u_codes = [sb.tile([P, HALF], U32, name=f"u_codes{h}", align_bytes=64) for h in range(halves)]
+        u_s = [sb.tile([P, HALF], U8, name=f"u_s{h}", align_bytes=64) for h in range(halves)]
+        hid = [sb.tile([P, HALF * PACK], BF16, name=f"hid{h}", align_bytes=64) for h in range(halves)]
+        hid_codes = [sb.tile([P, HALF], U32, name=f"hid_codes{h}", align_bytes=64) for h in range(halves)]
+        hid_s = [sb.tile([P, HALF], U8, name=f"hid_s{h}", align_bytes=64) for h in range(halves)]
+        magn = [sb.tile([P, N], F32, name=f"magn{h}") for h in range(halves)]
+        mean = [sb.tile([P, 1], F32, name=f"mean{h}") for h in range(halves)]
+        minus = [sb.tile([P, N], F32, name=f"minus{h}") for h in range(halves)]
+        res = [sb.tile([P, N], F32, name=f"res{h}") for h in range(halves)]
+        a_ps = [ps.tile([P, PACK, HALF], F32, name=f"a_ps{h}") for h in range(halves)]
+        p_ps = [ps.tile([P, N], F32, name=f"p_ps{h}") for h in range(halves)]
+
+        def pick(engine, dst, lst, h, i):
+            picked = windows[i].indirect(lst[:, h * cols : (h + 1) * cols])
+            if engine == "scalar":
+                nc.scalar.activation(dst[h][:, i, :], picked, ACT.Copy)
+            else:
+                nc.vector.tensor_copy(dst[h][:, i, :], picked)
+
+        def larger(h, lo, hi):
+            nc.vector.tensor_tensor(big[h][:, lo:hi, :], ga[h][:, lo:hi, :], gb[h][:, lo:hi, :], ALU.max)
+
+        def scale_round(h):
+            nc.vector.tensor_tensor(
+                u[h][:].rearrange("p (c e i) -> p c i e", e=2, i=PACK),
+                big[h][:].rearrange("p i (c e) -> p c i e", e=2),
+                factor[:].unsqueeze(1).unsqueeze(3).broadcast_to([P, HALF // 2, PACK, 2]),
+                ALU.mult,
+            )
+
+        def deal(copy, dst, src, run):
+            copy(
+                dst.rearrange("p (t c e) -> p c t e", t=PACK, e=run),
+                src.rearrange("p (c e t) -> p c t e", t=PACK, e=run),
+            )
+
+        def own_product(h):
+            for t in range(PACK):
+                nc.tensor.matmul_mx(
+                    out=a_ps[h][:, t, :],
+                    lhsT=w2_codes[:, t * P : (t + 1) * P].bitcast(E5M2),
+                    lhsT_scale=ws[:, t * P : (t + 1) * P],
+                    rhs=sx_codes[:, 2 * h * HALF : 2 * (h + 1) * HALF].bitcast(E2M1),
+                    rhs_scale=sx_s[:, h * HALF : (h + 1) * HALF],
+                    start=(t == 0),
+                    stop=False,
+                )
+
+        def picked_product(h):
+            nc.vector.quantize_mx(out=u_codes[h][:].bitcast(E4M3), scales=u_s[h][:], in_=u[h][:])
+            for t in range(PACK):
+                nc.tensor.matmul_mx(
+                    out=a_ps[h][:, t, :],
+                    lhsT=w_codes[:, t * P : (t + 1) * P].bitcast(E4M3),
+                    lhsT_scale=ws[W_ROW:P, t * P : (t + 1) * P],
+                    rhs=u_codes[h][:].bitcast(E4M3),
+                    rhs_scale=u_s[h][:],
+                    start=False,
+                    stop=(t == PACK - 1),
+                )
+
+        def relu(h):
+            lo = (LAG + h * HALF) * PACK
+            nc.scalar.activation(
+                ha[:, lo : lo + HALF * PACK].rearrange("p (j t) -> p j t", t=PACK),
+                a_ps[h][:].rearrange("p t j -> p j t"),
+                ACT.Relu,
+            )
+
+        def lagged(h):
+            lo = h * HALF * PACK
+            nc.vector.scalar_tensor_tensor(
+                hid[h][:], ha[:, lo : lo + HALF * PACK], -0.5, ha[:, lo + LAG * PACK : lo + (LAG + HALF) * PACK], ALU.mult, ALU.add
+            )
+
+        def second_product(h):
+            nc.vector.quantize_mx(out=hid_codes[h][:].bitcast(E5M2), scales=hid_s[h][:], in_=hid[h][:])
+            nc.tensor.matmul_mx(
+                out=p_ps[h][:],
+                lhsT=hid_codes[h][:].bitcast(E5M2),
+                lhsT_scale=hid_s[h][:],
+                rhs=wb_codes[:].bitcast(E2M1),
+                rhs_scale=wb_s[:],
+                start=True,
+                stop=True,
+            )
+
+        def finish(h):
+            nc.scalar.activation(magn[h][:], p_ps[h][:], ACT.Abs, scale=1.0 / N, accum_out=mean[h][:])
+            nc.scalar.activation(minus[h][:], resid[:, h, :], ACT.Identity, scale=0.3, bias=mean[h][:])
+            nc.vector.scalar_tensor_tensor(res[h][:], p_ps[h][:], mean[h][:], minus[h][:], ALU.max, ALU.subtract)
+            nc.sync.dma_start(out=out[h * HALF : (h + 1) * HALF, :], in_=res[h][:])
+
+        for i in range(2):
+            for h in range(halves):
+                pick("scalar", ga, list_a, h, i)
+                pick("vector", gb, list_b, h, i)
+        for h in range(halves):
+            larger(h, 0, 2)
+        for i in range(2, 4):
+            pick("scalar", ga, list_a, 0, i)
+            pick("vector", gb, list_b, 0, i)
+        larger(0, 2, 4)
+        deal(nc.vector.tensor_copy, ws[:], ws_raw[:], 16)
+        deal(nc.scalar.copy, w2_codes[:], w2_raw[:], 4)
+        deal(nc.scalar.copy, w_codes[:], w_raw[:], 4)
+        scale_round(0)
+        own_product(0)
+        picked_product(0)
+        own_product(1)
+        for i in range(2, 4):
+            pick("scalar", ga, list_a, 1, i)
+            pick("vector", gb, list_b, 1, i)
+        larger(1, 2, 4)
+        relu(0)
+        scale_round(1)
+        picked_product(1)
+        lagged(0)
+        relu(1)
+        second_product(0)
+        lagged(1)
+        second_product(1)
+        finish(0)
+        finish(1)

@@ -21,7 +21,6 @@ P = 128
 PACK = 4
 HALF = 128
 LAG = 2
-W_ROW = 4
 
 
 def tile_list_sum_largerpicks_own_lagged_rowabove_kernel(
@@ -32,6 +31,7 @@ def tile_list_sum_largerpicks_own_lagged_rowabove_kernel(
     cols = HALF // 16
     with ExitStack() as ctx:
         sb = ctx.enter_context(tc.tile_pool(name="sb", bufs=1))
+        shared = ctx.enter_context(tc.tile_pool(name="shared", bufs=1))
         ps = ctx.enter_context(tc.psum_pool(name="ps", bufs=1))
 
         list_a = sb.tile([P, J // 16], U16, name="list_a")
@@ -41,54 +41,70 @@ def tile_list_sum_largerpicks_own_lagged_rowabove_kernel(
         x23 = sb.tile([P, 2, T], F32, name="x23")
         windows = [x0[:], x1[:], x23[:, 0, :], x23[:, 1, :]]
         factor = sb.tile([P, PACK], F32, name="factor")
-        w_raw = sb.tile([P, R], U32, name="w_raw")
-        w2_raw = sb.tile([P, R], U32, name="w2_raw")
-        ws_raw = sb.tile([P, R], U8, name="ws_raw")
+        w_raw = shared.tile([P, R], U32, name="w_raw", offset=4096, align_bytes=64)
+        w2_raw = shared.tile([P, R], U32, name="w2_raw", offset=6144, align_bytes=64)
+        raw = sb.tile([P, 2 * R], U8, name="raw")
+        scales = sb.tile([P, 2 * R + J], U8, name="scales", align_bytes=64)
+        w2s, ws = scales[:, 0:R], scales[:, R : 2 * R]
+        sx_s = scales[:, 2 * R :]
+        wb_s = shared.tile([P, N], U8, name="wb_s", offset=512, align_bytes=64)
         w_codes = sb.tile([P, R], U32, name="w_codes", align_bytes=64)
         w2_codes = sb.tile([P, R], U32, name="w2_codes", align_bytes=64)
-        ws = sb.tile([P, R], U8, name="ws", align_bytes=64)
         sx_codes = sb.tile([P, 2 * J], U8, name="sx_codes", align_bytes=64)
-        sx_s = sb.tile([P, J], U8, name="sx_s", align_bytes=64)
-        wb_codes = sb.tile([P, 2 * N], U8, name="wb_codes", align_bytes=64)
-        wb_s = sb.tile([P, N], U8, name="wb_s", align_bytes=64)
-        resid = sb.tile([P, halves, N], F32, name="resid")
+        wb_codes = shared.tile([P, 2 * N], U8, name="wb_codes", offset=0, align_bytes=64)
+        resid = shared.tile([P, halves, N], F32, name="resid", offset=1024, align_bytes=64)
+        zeros = sb.tile([P, LAG * PACK], F32, name="zeros")
         ha = sb.tile([P, (J + LAG) * PACK], F32, name="ha")
 
-        def load_scale_row(queue, tile, first, scales, r):
-            queue.dma_start(out=tile[:].bitcast(I32)[first + r : P : 32, :], in_=scales[0, r:16:4, :].bitcast(I32))
+        ga = [[None, None], [None, None]]
+        gb = [[None, None], [None, None]]
+        for h in range(halves):
+            ga[h][0] = sb.tile([P, 2, HALF], F32, name=f"ga{h}0")
+            gb[h][0] = sb.tile([P, 2, HALF], F32, name=f"gb{h}0")
+        ga[0][1] = shared.tile([P, 2, HALF], F32, name="ga01", offset=0, align_bytes=64)
+        gb[0][1] = shared.tile([P, 2, HALF], F32, name="gb01", offset=1024, align_bytes=64)
+        ga[1][1] = sb.tile([P, 2, HALF], F32, name="ga11")
+        gb[1][1] = sb.tile([P, 2, HALF], F32, name="gb11")
 
-        nc.vector.memset(ws_raw[:].bitcast(U32), 0)
-        nc.gpsimd.memset(sx_s[:].bitcast(U32), 0)
-        nc.vector.memset(wb_s[:].bitcast(U32), 0)
-        nc.vector.memset(ha[:, 0 : LAG * PACK], 0.0)
+        nc.vector.memset(zeros[:], 0.0)
+        for lo, hi in ((32, 64), (64, P)):
+            nc.vector.memset(raw[:].bitcast(U32)[lo:hi, :], 0)
+        nc.scalar.activation(ha[:, 0 : LAG * PACK], zeros[:], ACT.Copy)
 
         planes = xf.rearrange("(p i) t -> p i t", i=PACK)
+        for n, src in enumerate((w2_scales, w_scales)):
+            nc.sync.dma_start(
+                out=raw[:, n * R : (n + 1) * R].bitcast(I32)[0:32, :],
+                in_=src.bitcast(I32).broadcast_to([2, 16, R // 4]),
+            )
+        nc.sync.dma_start(out=x0[:], in_=planes[:, 0, :])
         nc.sync.dma_start(list_a[:], offs)
         nc.sync.dma_start(list_b[:], offs2)
-        nc.sync.dma_start(out=x0[:], in_=planes[:, 0, :])
+        nc.sync.dma_start(out=sx_s.bitcast(I32)[0:16, :], in_=sx_scales[0].bitcast(I32))
         nc.sync.dma_start(out=x1[:], in_=planes[:, 1, :])
-        for r in range(3):
-            load_scale_row(nc.sync, ws_raw, 0, w2_scales, r)
         nc.sync.dma_start(out=x23[:], in_=planes[:, 2:4, :])
-        load_scale_row(nc.sync, ws_raw, 0, w2_scales, 3)
-        for r in range(4):
-            load_scale_row(nc.sync, ws_raw, W_ROW, w_scales, r)
+        nc.sync.dma_start(out=factor[:], in_=fk.rearrange("(p i) o -> p (i o)", i=PACK))
         nc.sync.dma_start(out=w2_raw[:].bitcast(I32), in_=w2_words[0].rearrange("p n t -> p (n t)").bitcast(I32))
         nc.sync.dma_start(out=w_raw[:].bitcast(I32), in_=w_words[0].rearrange("p n t -> p (n t)").bitcast(I32))
         nc.sync.dma_start(out=sx_codes[:].bitcast(I32), in_=sx_words[0].bitcast(I32))
-        nc.sync.dma_start(out=wb_codes[:].bitcast(I32), in_=wb_words[0].bitcast(I32))
-        for r in range(4):
-            load_scale_row(nc.sync, wb_s, 0, wb_scales, r)
-        nc.sync.dma_start(out=resid[:], in_=rs.rearrange("(h p) n -> p h n", p=P))
-        nc.gpsimd.dma_start(out=factor[:], in_=fk.rearrange("(p i) o -> p (i o)", i=PACK))
-        for r in range(4):
-            load_scale_row(nc.gpsimd, sx_s, 0, sx_scales, r)
+        nc.vector.tensor_copy(
+            scales[:, 0 : 2 * R].rearrange("p (a t m) -> p a m t", a=2, t=PACK),
+            raw[:].rearrange("p (a m t) -> p a m t", a=2, t=PACK),
+        )
+        rows = scales[:].bitcast(I32)
+        for q in range(1, 4):
+            nc.sync.dma_start(out=rows[32 * q : 32 * q + 4, :], in_=rows[4 * q : 4 * q + 4, :])
 
-        ga = [sb.tile([P, PACK, HALF], F32, name=f"ga{h}") for h in range(halves)]
-        gb = [sb.tile([P, PACK, HALF], F32, name=f"gb{h}") for h in range(halves)]
-        big = [sb.tile([P, PACK, HALF], F32, name=f"big{h}") for h in range(halves)]
-        u = [sb.tile([P, HALF * PACK], BF16, name=f"u{h}", align_bytes=64) for h in range(halves)]
-        u_codes = [sb.tile([P, HALF], U32, name=f"u_codes{h}", align_bytes=64) for h in range(halves)]
+        bigs = sb.tile([P, 6, HALF], F32, name="bigs")
+        big = [bigs[:, 2:6, :], bigs[:, 0:4, :]]
+        u = [
+            shared.tile([P, HALF * PACK], BF16, name="u0", offset=6144, align_bytes=64),
+            sb.tile([P, HALF * PACK], BF16, name="u1", align_bytes=64),
+        ]
+        u_codes = [
+            shared.tile([P, HALF], U32, name="u_codes0", offset=4096, align_bytes=64),
+            sb.tile([P, HALF], U32, name="u_codes1", align_bytes=64),
+        ]
         u_s = [sb.tile([P, HALF], U8, name=f"u_s{h}", align_bytes=64) for h in range(halves)]
         hid = [sb.tile([P, HALF * PACK], BF16, name=f"hid{h}", align_bytes=64) for h in range(halves)]
         hid_codes = [sb.tile([P, HALF], U32, name=f"hid_codes{h}", align_bytes=64) for h in range(halves)]
@@ -103,46 +119,45 @@ def tile_list_sum_largerpicks_own_lagged_rowabove_kernel(
         def pick(engine, dst, lst, h, i):
             picked = windows[i].indirect(lst[:, h * cols : (h + 1) * cols])
             if engine == "scalar":
-                nc.scalar.activation(dst[h][:, i, :], picked, ACT.Copy)
+                nc.scalar.activation(dst[h][i // 2][:, i % 2, :], picked, ACT.Copy)
             else:
-                nc.vector.tensor_copy(dst[h][:, i, :], picked)
+                nc.vector.tensor_copy(dst[h][i // 2][:, i % 2, :], picked)
 
         def larger(h, lo, hi):
-            nc.vector.tensor_tensor(big[h][:, lo:hi, :], ga[h][:, lo:hi, :], gb[h][:, lo:hi, :], ALU.max)
+            nc.vector.tensor_tensor(big[h][:, lo:hi, :], ga[h][lo // 2][:], gb[h][lo // 2][:], ALU.max)
 
         def scale_round(h):
             nc.vector.tensor_tensor(
                 u[h][:].rearrange("p (c e i) -> p c i e", e=2, i=PACK),
-                big[h][:].rearrange("p i (c e) -> p c i e", e=2),
+                big[h].rearrange("p i (c e) -> p c i e", e=2),
                 factor[:].unsqueeze(1).unsqueeze(3).broadcast_to([P, HALF // 2, PACK, 2]),
                 ALU.mult,
             )
 
-        def deal(copy, dst, src, run):
-            copy(
-                dst.rearrange("p (t c e) -> p c t e", t=PACK, e=run),
-                src.rearrange("p (c e t) -> p c t e", t=PACK, e=run),
-            )
+        def deal(copy, dst, src):
+            copy(dst.rearrange("p (t m) -> p m t", t=PACK), src.rearrange("p (m t) -> p m t", t=PACK))
 
         def own_product(h):
             for t in range(PACK):
                 nc.tensor.matmul_mx(
                     out=a_ps[h][:, t, :],
                     lhsT=w2_codes[:, t * P : (t + 1) * P].bitcast(E5M2),
-                    lhsT_scale=ws[:, t * P : (t + 1) * P],
+                    lhsT_scale=w2s[:, t * P : (t + 1) * P],
                     rhs=sx_codes[:, 2 * h * HALF : 2 * (h + 1) * HALF].bitcast(E2M1),
                     rhs_scale=sx_s[:, h * HALF : (h + 1) * HALF],
                     start=(t == 0),
                     stop=False,
                 )
 
-        def picked_product(h):
+        def quantise_u(h):
             nc.vector.quantize_mx(out=u_codes[h][:].bitcast(E4M3), scales=u_s[h][:], in_=u[h][:])
+
+        def picked_product(h):
             for t in range(PACK):
                 nc.tensor.matmul_mx(
                     out=a_ps[h][:, t, :],
                     lhsT=w_codes[:, t * P : (t + 1) * P].bitcast(E4M3),
-                    lhsT_scale=ws[W_ROW:P, t * P : (t + 1) * P],
+                    lhsT_scale=ws[:, t * P : (t + 1) * P],
                     rhs=u_codes[h][:].bitcast(E4M3),
                     rhs_scale=u_s[h][:],
                     start=False,
@@ -187,24 +202,30 @@ def tile_list_sum_largerpicks_own_lagged_rowabove_kernel(
                 pick("vector", gb, list_b, h, i)
         for h in range(halves):
             larger(h, 0, 2)
-        for i in range(2, 4):
-            pick("scalar", ga, list_a, 0, i)
-            pick("vector", gb, list_b, 0, i)
-        larger(0, 2, 4)
-        deal(nc.vector.tensor_copy, ws[:], ws_raw[:], 16)
-        deal(nc.scalar.copy, w2_codes[:], w2_raw[:], 4)
-        deal(nc.scalar.copy, w_codes[:], w_raw[:], 4)
-        scale_round(0)
-        own_product(0)
-        picked_product(0)
-        own_product(1)
+        pick("scalar", ga, list_a, 0, 2)
+        pick("scalar", ga, list_a, 0, 3)
+        pick("scalar", gb, list_b, 0, 2)
+        pick("vector", gb, list_b, 0, 3)
         for i in range(2, 4):
             pick("scalar", ga, list_a, 1, i)
-            pick("vector", gb, list_b, 1, i)
+            pick("scalar", gb, list_b, 1, i)
+        deal(nc.vector.tensor_copy, w2_codes[:].bitcast(I32), w2_raw[:].bitcast(I32))
+        larger(0, 2, 4)
+        nc.sync.dma_start(out=wb_codes[:].bitcast(I32), in_=wb_words[0].bitcast(I32))
+        for r in range(4):
+            nc.sync.dma_start(out=wb_s[:].bitcast(I32)[r:P:32, :], in_=wb_scales[0, r:16:4, :].bitcast(I32))
+        nc.sync.dma_start(out=resid[:], in_=rs.rearrange("(h p) n -> p h n", p=P))
+        scale_round(0)
+        deal(nc.vector.tensor_copy, w_codes[:].bitcast(I32), w_raw[:].bitcast(I32))
+        quantise_u(0)
+        own_product(0)
+        own_product(1)
+        picked_product(0)
         larger(1, 2, 4)
-        relu(0)
         scale_round(1)
+        quantise_u(1)
         picked_product(1)
+        relu(0)
         lagged(0)
         relu(1)
         second_product(0)

@@ -28,7 +28,6 @@ def tile_list_sum_largerpicks_own_lagged_rowabove_kernel(
 ):
     nc = tc.nc
     halves = J // HALF
-    cols = HALF // 16
     with ExitStack() as ctx:
         sb = ctx.enter_context(tc.tile_pool(name="sb", bufs=1))
         shared = ctx.enter_context(tc.tile_pool(name="shared", bufs=1))
@@ -64,7 +63,7 @@ def tile_list_sum_largerpicks_own_lagged_rowabove_kernel(
         ga[0][1] = shared.tile([P, 2, HALF], F32, name="ga01", offset=0, align_bytes=64)
         gb[0][1] = shared.tile([P, 2, HALF], F32, name="gb01", offset=1024, align_bytes=64)
         ga[1][1] = sb.tile([P, 2, HALF], F32, name="ga11")
-        gb[1][1] = sb.tile([P, 2, HALF], F32, name="gb11")
+        gb[1][1] = shared.tile([P, 2, HALF], F32, name="gb11", offset=4096, align_bytes=64)
 
         nc.vector.memset(zeros[:], 0.0)
         for lo, hi in ((32, 64), (64, P)):
@@ -101,10 +100,7 @@ def tile_list_sum_largerpicks_own_lagged_rowabove_kernel(
             shared.tile([P, HALF * PACK], BF16, name="u0", offset=6144, align_bytes=64),
             sb.tile([P, HALF * PACK], BF16, name="u1", align_bytes=64),
         ]
-        u_codes = [
-            shared.tile([P, HALF], U32, name="u_codes0", offset=4096, align_bytes=64),
-            sb.tile([P, HALF], U32, name="u_codes1", align_bytes=64),
-        ]
+        u_codes = [sb.tile([P, HALF], U32, name=f"u_codes{h}", align_bytes=64) for h in range(halves)]
         u_s = [sb.tile([P, HALF], U8, name=f"u_s{h}", align_bytes=64) for h in range(halves)]
         hid = [sb.tile([P, HALF * PACK], BF16, name=f"hid{h}", align_bytes=64) for h in range(halves)]
         hid_codes = [sb.tile([P, HALF], U32, name=f"hid_codes{h}", align_bytes=64) for h in range(halves)]
@@ -116,21 +112,23 @@ def tile_list_sum_largerpicks_own_lagged_rowabove_kernel(
         a_ps = [ps.tile([P, PACK, HALF], F32, name=f"a_ps{h}") for h in range(halves)]
         p_ps = [ps.tile([P, N], F32, name=f"p_ps{h}") for h in range(halves)]
 
-        def pick(engine, dst, lst, h, i):
-            picked = windows[i].indirect(lst[:, h * cols : (h + 1) * cols])
+        def pick(engine, dst, lst, h, i, lo=0, hi=HALF):
+            picked = windows[i].indirect(lst[:, (h * HALF + lo) // 16 : (h * HALF + hi) // 16])
             if engine == "scalar":
-                nc.scalar.activation(dst[h][i // 2][:, i % 2, :], picked, ACT.Copy)
+                nc.scalar.activation(dst[h][i // 2][:, i % 2, lo:hi], picked, ACT.Copy)
             else:
-                nc.vector.tensor_copy(dst[h][i // 2][:, i % 2, :], picked)
+                nc.vector.tensor_copy(dst[h][i // 2][:, i % 2, lo:hi], picked)
 
-        def larger(h, lo, hi):
-            nc.vector.tensor_tensor(big[h][:, lo:hi, :], ga[h][lo // 2][:], gb[h][lo // 2][:], ALU.max)
-
-        def scale_round(h):
+        def larger(h, pair, lo=0, hi=HALF):
             nc.vector.tensor_tensor(
-                u[h][:].rearrange("p (c e i) -> p c i e", e=2, i=PACK),
-                big[h].rearrange("p i (c e) -> p c i e", e=2),
-                factor[:].unsqueeze(1).unsqueeze(3).broadcast_to([P, HALF // 2, PACK, 2]),
+                big[h][:, 2 * pair : 2 * pair + 2, lo:hi], ga[h][pair][:, :, lo:hi], gb[h][pair][:, :, lo:hi], ALU.max
+            )
+
+        def scale_round(h, lo=0, hi=HALF):
+            nc.vector.tensor_tensor(
+                u[h][:, lo * PACK : hi * PACK].rearrange("p (c e i) -> p c i e", e=2, i=PACK),
+                big[h][:, :, lo:hi].rearrange("p i (c e) -> p c i e", e=2),
+                factor[:].unsqueeze(1).unsqueeze(3).broadcast_to([P, (hi - lo) // 2, PACK, 2]),
                 ALU.mult,
             )
 
@@ -149,8 +147,10 @@ def tile_list_sum_largerpicks_own_lagged_rowabove_kernel(
                     stop=False,
                 )
 
-        def quantise_u(h):
-            nc.vector.quantize_mx(out=u_codes[h][:].bitcast(E4M3), scales=u_s[h][:], in_=u[h][:])
+        def quantise(codes, plane, values, fmt, lo=0, hi=HALF):
+            nc.vector.quantize_mx(
+                out=codes[:, lo:hi].bitcast(fmt), scales=plane[:, lo:hi], in_=values[:, lo * PACK : hi * PACK]
+            )
 
         def picked_product(h):
             for t in range(PACK):
@@ -164,22 +164,26 @@ def tile_list_sum_largerpicks_own_lagged_rowabove_kernel(
                     stop=(t == PACK - 1),
                 )
 
-        def relu(h):
-            lo = (LAG + h * HALF) * PACK
+        def relu(h, lo=0, hi=HALF):
+            first = LAG + h * HALF
             nc.scalar.activation(
-                ha[:, lo : lo + HALF * PACK].rearrange("p (j t) -> p j t", t=PACK),
-                a_ps[h][:].rearrange("p t j -> p j t"),
+                ha[:, (first + lo) * PACK : (first + hi) * PACK].rearrange("p (j t) -> p j t", t=PACK),
+                a_ps[h][:, :, lo:hi].rearrange("p t j -> p j t"),
                 ACT.Relu,
             )
 
-        def lagged(h):
-            lo = h * HALF * PACK
+        def lagged(h, lo=0, hi=HALF):
+            first = h * HALF
             nc.vector.scalar_tensor_tensor(
-                hid[h][:], ha[:, lo : lo + HALF * PACK], -0.5, ha[:, lo + LAG * PACK : lo + (LAG + HALF) * PACK], ALU.mult, ALU.add
+                hid[h][:, lo * PACK : hi * PACK],
+                ha[:, (first + lo) * PACK : (first + hi) * PACK],
+                -0.5,
+                ha[:, (first + lo + LAG) * PACK : (first + hi + LAG) * PACK],
+                ALU.mult,
+                ALU.add,
             )
 
         def second_product(h):
-            nc.vector.quantize_mx(out=hid_codes[h][:].bitcast(E5M2), scales=hid_s[h][:], in_=hid[h][:])
             nc.tensor.matmul_mx(
                 out=p_ps[h][:],
                 lhsT=hid_codes[h][:].bitcast(E5M2),
@@ -196,40 +200,58 @@ def tile_list_sum_largerpicks_own_lagged_rowabove_kernel(
             nc.vector.scalar_tensor_tensor(res[h][:], p_ps[h][:], mean[h][:], minus[h][:], ALU.max, ALU.subtract)
             nc.sync.dma_start(out=out[h * HALF : (h + 1) * HALF, :], in_=res[h][:])
 
+        quarters = ((0, HALF // 2), (HALF // 2, HALF))
         for i in range(2):
             for h in range(halves):
                 pick("scalar", ga, list_a, h, i)
                 pick("vector", gb, list_b, h, i)
         for h in range(halves):
-            larger(h, 0, 2)
-        pick("scalar", ga, list_a, 0, 2)
-        pick("scalar", ga, list_a, 0, 3)
-        pick("scalar", gb, list_b, 0, 2)
-        pick("vector", gb, list_b, 0, 3)
+            larger(h, 0)
+        for i in range(2, 4):
+            pick("scalar", ga, list_a, 0, i)
+            pick("vector", gb, list_b, 0, i)
         for i in range(2, 4):
             pick("scalar", ga, list_a, 1, i)
-            pick("scalar", gb, list_b, 1, i)
+        larger(0, 1)
         deal(nc.vector.tensor_copy, w2_codes[:].bitcast(I32), w2_raw[:].bitcast(I32))
-        larger(0, 2, 4)
         nc.sync.dma_start(out=wb_codes[:].bitcast(I32), in_=wb_words[0].bitcast(I32))
         for r in range(4):
             nc.sync.dma_start(out=wb_s[:].bitcast(I32)[r:P:32, :], in_=wb_scales[0, r:16:4, :].bitcast(I32))
         nc.sync.dma_start(out=resid[:], in_=rs.rearrange("(h p) n -> p h n", p=P))
         scale_round(0)
-        deal(nc.vector.tensor_copy, w_codes[:].bitcast(I32), w_raw[:].bitcast(I32))
-        quantise_u(0)
+        deal(nc.scalar.copy, w_codes[:], w_raw[:])
+        quantise(u_codes[0], u_s[0], u[0], E4M3)
         own_product(0)
         own_product(1)
         picked_product(0)
-        larger(1, 2, 4)
-        scale_round(1)
-        quantise_u(1)
+        for lo, hi in quarters:
+            for i in range(2, 4):
+                pick("scalar", gb, list_b, 1, i, lo, hi)
+        for lo, hi in quarters:
+            larger(1, 1, lo, hi)
+        for lo, hi in quarters:
+            scale_round(1, lo, hi)
+        for lo, hi in quarters:
+            quantise(u_codes[1], u_s[1], u[1], E4M3, lo, hi)
         picked_product(1)
         relu(0)
         lagged(0)
-        relu(1)
+        quantise(hid_codes[0], hid_s[0], hid[0], E5M2)
         second_product(0)
-        lagged(1)
+        for lo, hi in quarters:
+            relu(1, lo, hi)
+        for lo, hi in quarters:
+            lagged(1, lo, hi)
+        for lo, hi in quarters:
+            quantise(hid_codes[1], hid_s[1], hid[1], E5M2, lo, hi)
         second_product(1)
         finish(0)
-        finish(1)
+        nc.scalar.activation(magn[1][:], p_ps[1][:], ACT.Abs, scale=1.0 / N, accum_out=mean[1][:])
+        sides = (slice(0, N // 2), slice(N // 2, N))
+        for side in sides:
+            nc.vector.tensor_scalar(minus[1][:, side], resid[:, 1, side], 0.3, mean[1][:], ALU.mult, ALU.add)
+        for side in sides:
+            nc.vector.scalar_tensor_tensor(
+                res[1][:, side], p_ps[1][:, side], mean[1][:], minus[1][:, side], ALU.max, ALU.subtract
+            )
+            nc.sync.dma_start(out=out[HALF:J, side], in_=res[1][:, side])

from contextlib import ExitStack

import concourse.mybir as mybir

K, T, J, R, F, N = 512, 512, 256, 512, 512, 256
FLOPS = 2 * (K * R * J + F * R * J + R * J * N)

F32 = mybir.dt.float32
BF16 = mybir.dt.bfloat16
I32 = mybir.dt.int32
U32 = mybir.dt.uint32
U16 = mybir.dt.uint16
U8 = mybir.dt.uint8
E4M3 = mybir.dt.float8_e4m3fn_x4
E5M2 = mybir.dt.float8_e5m2_x4
E2M1 = mybir.dt.float4_e2m1fn_x4
ALU = mybir.AluOpType
ACT = mybir.ActivationFunctionType

P = 128
PACK = 4
HALF = 128
LAG = 2


def tile_list_sum_largerpicks_own_lagged_rowabove_kernel(
    tc, xf, fk, w_words, w_scales, sx_words, sx_scales, w2_words, w2_scales, wb_words, wb_scales, rs, offs, offs2, out
):
    nc = tc.nc
    halves = J // HALF
    with ExitStack() as ctx:
        sb = ctx.enter_context(tc.tile_pool(name="sb", bufs=1))
        shared = ctx.enter_context(tc.tile_pool(name="shared", bufs=1))
        ps = ctx.enter_context(tc.psum_pool(name="ps", bufs=1))

        list_a = sb.tile([P, J // 16], U16, name="list_a")
        list_b = sb.tile([P, J // 16], U16, name="list_b")
        x0 = sb.tile([P, T], F32, name="x0")
        x1 = sb.tile([P, T], F32, name="x1")
        x23 = sb.tile([P, 2, T], F32, name="x23")
        windows = [x0[:], x1[:], x23[:, 0, :], x23[:, 1, :]]
        factor = sb.tile([P, PACK], F32, name="factor")
        w_raw = shared.tile([P, R], U32, name="w_raw", offset=4096, align_bytes=64)
        w2_raw = shared.tile([P, R], U32, name="w2_raw", offset=6144, align_bytes=64)
        raw = sb.tile([P, 2 * R], U8, name="raw")
        scales = sb.tile([P, 2 * R + J], U8, name="scales", align_bytes=64)
        w2s, ws = scales[:, 0:R], scales[:, R : 2 * R]
        sx_s = scales[:, 2 * R :]
        wb_s = shared.tile([P, N], U8, name="wb_s", offset=512, align_bytes=64)
        w_codes = sb.tile([P, R], U32, name="w_codes", align_bytes=64)
        w2_codes = sb.tile([P, R], U32, name="w2_codes", align_bytes=64)
        sx_codes = sb.tile([P, 2 * J], U8, name="sx_codes", align_bytes=64)
        wb_codes = shared.tile([P, 2 * N], U8, name="wb_codes", offset=0, align_bytes=64)
        resid = shared.tile([P, halves, N], F32, name="resid", offset=1024, align_bytes=64)
        zeros = sb.tile([P, LAG * PACK], F32, name="zeros")
        ha = sb.tile([P, (J + LAG) * PACK], F32, name="ha")

        ga = [[None, None], [None, None]]
        gb = [[None, None], [None, None]]
        for h in range(halves):
            ga[h][0] = sb.tile([P, 2, HALF], F32, name=f"ga{h}0")
            gb[h][0] = sb.tile([P, 2, HALF], F32, name=f"gb{h}0")
        ga[0][1] = shared.tile([P, 2, HALF], F32, name="ga01", offset=0, align_bytes=64)
        gb[0][1] = shared.tile([P, 2, HALF], F32, name="gb01", offset=1024, align_bytes=64)
        ga[1][1] = sb.tile([P, 2, HALF], F32, name="ga11")
        gb[1][1] = shared.tile([P, 2, HALF], F32, name="gb11", offset=4096, align_bytes=64)

        nc.vector.memset(zeros[:], 0.0)
        for lo, hi in ((32, 64), (64, P)):
            nc.vector.memset(raw[:].bitcast(U32)[lo:hi, :], 0)
        nc.scalar.activation(ha[:, 0 : LAG * PACK], zeros[:], ACT.Copy)

        planes = xf.rearrange("(p i) t -> p i t", i=PACK)
        for n, src in enumerate((w2_scales, w_scales)):
            nc.sync.dma_start(
                out=raw[:, n * R : (n + 1) * R].bitcast(I32)[0:32, :],
                in_=src.bitcast(I32).broadcast_to([2, 16, R // 4]),
            )
        nc.sync.dma_start(out=x0[:], in_=planes[:, 0, :])
        nc.sync.dma_start(list_a[:], offs)
        nc.sync.dma_start(list_b[:], offs2)
        nc.sync.dma_start(out=sx_s.bitcast(I32)[0:16, :], in_=sx_scales[0].bitcast(I32))
        nc.sync.dma_start(out=x1[:], in_=planes[:, 1, :])
        nc.sync.dma_start(out=x23[:], in_=planes[:, 2:4, :])
        nc.sync.dma_start(out=factor[:], in_=fk.rearrange("(p i) o -> p (i o)", i=PACK))
        nc.sync.dma_start(out=w2_raw[:].bitcast(I32), in_=w2_words[0].rearrange("p n t -> p (n t)").bitcast(I32))
        nc.sync.dma_start(out=w_raw[:].bitcast(I32), in_=w_words[0].rearrange("p n t -> p (n t)").bitcast(I32))
        nc.sync.dma_start(out=sx_codes[:].bitcast(I32), in_=sx_words[0].bitcast(I32))
        nc.vector.tensor_copy(
            scales[:, 0 : 2 * R].rearrange("p (a t m) -> p a m t", a=2, t=PACK),
            raw[:].rearrange("p (a m t) -> p a m t", a=2, t=PACK),
        )
        rows = scales[:].bitcast(I32)
        for q in range(1, 4):
            nc.sync.dma_start(out=rows[32 * q : 32 * q + 4, :], in_=rows[4 * q : 4 * q + 4, :])

        bigs = sb.tile([P, 6, HALF], F32, name="bigs")
        big = [bigs[:, 2:6, :], bigs[:, 0:4, :]]
        u = [
            shared.tile([P, HALF * PACK], BF16, name="u0", offset=6144, align_bytes=64),
            sb.tile([P, HALF * PACK], BF16, name="u1", align_bytes=64),
        ]
        u_codes = [sb.tile([P, HALF], U32, name=f"u_codes{h}", align_bytes=64) for h in range(halves)]
        u_s = [sb.tile([P, HALF], U8, name=f"u_s{h}", align_bytes=64) for h in range(halves)]
        hid = [sb.tile([P, HALF * PACK], BF16, name=f"hid{h}", align_bytes=64) for h in range(halves)]
        hid_codes = [sb.tile([P, HALF], U32, name=f"hid_codes{h}", align_bytes=64) for h in range(halves)]
        hid_s = [sb.tile([P, HALF], U8, name=f"hid_s{h}", align_bytes=64) for h in range(halves)]
        magn = [sb.tile([P, N], F32, name=f"magn{h}") for h in range(halves)]
        mean = [sb.tile([P, 1], F32, name=f"mean{h}") for h in range(halves)]
        minus = [sb.tile([P, N], F32, name=f"minus{h}") for h in range(halves)]
        res = [sb.tile([P, N], F32, name=f"res{h}") for h in range(halves)]
        a_ps = [ps.tile([P, PACK, HALF], F32, name=f"a_ps{h}") for h in range(halves)]
        p_ps = [ps.tile([P, N], F32, name=f"p_ps{h}") for h in range(halves)]

        def pick(engine, dst, lst, h, i, lo=0, hi=HALF):
            picked = windows[i].indirect(lst[:, (h * HALF + lo) // 16 : (h * HALF + hi) // 16])
            if engine == "scalar":
                nc.scalar.activation(dst[h][i // 2][:, i % 2, lo:hi], picked, ACT.Copy)
            else:
                nc.vector.tensor_copy(dst[h][i // 2][:, i % 2, lo:hi], picked)

        def larger(h, pair, lo=0, hi=HALF):
            nc.vector.tensor_tensor(
                big[h][:, 2 * pair : 2 * pair + 2, lo:hi], ga[h][pair][:, :, lo:hi], gb[h][pair][:, :, lo:hi], ALU.max
            )

        def scale_round(h, lo=0, hi=HALF):
            nc.vector.tensor_tensor(
                u[h][:, lo * PACK : hi * PACK].rearrange("p (c e i) -> p c i e", e=2, i=PACK),
                big[h][:, :, lo:hi].rearrange("p i (c e) -> p c i e", e=2),
                factor[:].unsqueeze(1).unsqueeze(3).broadcast_to([P, (hi - lo) // 2, PACK, 2]),
                ALU.mult,
            )

        def deal(copy, dst, src):
            copy(dst.rearrange("p (t m) -> p m t", t=PACK), src.rearrange("p (m t) -> p m t", t=PACK))

        def own_product(h):
            for t in range(PACK):
                nc.tensor.matmul_mx(
                    out=a_ps[h][:, t, :],
                    lhsT=w2_codes[:, t * P : (t + 1) * P].bitcast(E5M2),
                    lhsT_scale=w2s[:, t * P : (t + 1) * P],
                    rhs=sx_codes[:, 2 * h * HALF : 2 * (h + 1) * HALF].bitcast(E2M1),
                    rhs_scale=sx_s[:, h * HALF : (h + 1) * HALF],
                    start=(t == 0),
                    stop=False,
                )

        def quantise(codes, plane, values, fmt, lo=0, hi=HALF):
            nc.vector.quantize_mx(
                out=codes[:, lo:hi].bitcast(fmt), scales=plane[:, lo:hi], in_=values[:, lo * PACK : hi * PACK]
            )

        def picked_product(h):
            for t in range(PACK):
                nc.tensor.matmul_mx(
                    out=a_ps[h][:, t, :],
                    lhsT=w_codes[:, t * P : (t + 1) * P].bitcast(E4M3),
                    lhsT_scale=ws[:, t * P : (t + 1) * P],
                    rhs=u_codes[h][:].bitcast(E4M3),
                    rhs_scale=u_s[h][:],
                    start=False,
                    stop=(t == PACK - 1),
                )

        def relu(h, lo=0, hi=HALF):
            first = LAG + h * HALF
            nc.scalar.activation(
                ha[:, (first + lo) * PACK : (first + hi) * PACK].rearrange("p (j t) -> p j t", t=PACK),
                a_ps[h][:, :, lo:hi].rearrange("p t j -> p j t"),
                ACT.Relu,
            )

        def lagged(h, lo=0, hi=HALF):
            first = h * HALF
            nc.vector.scalar_tensor_tensor(
                hid[h][:, lo * PACK : hi * PACK],
                ha[:, (first + lo) * PACK : (first + hi) * PACK],
                -0.5,
                ha[:, (first + lo + LAG) * PACK : (first + hi + LAG) * PACK],
                ALU.mult,
                ALU.add,
            )

        def second_product(h):
            nc.tensor.matmul_mx(
                out=p_ps[h][:],
                lhsT=hid_codes[h][:].bitcast(E5M2),
                lhsT_scale=hid_s[h][:],
                rhs=wb_codes[:].bitcast(E2M1),
                rhs_scale=wb_s[:],
                start=True,
                stop=True,
            )

        def finish(h):
            nc.scalar.activation(magn[h][:], p_ps[h][:], ACT.Abs, scale=1.0 / N, accum_out=mean[h][:])
            nc.scalar.activation(minus[h][:], resid[:, h, :], ACT.Identity, scale=0.3, bias=mean[h][:])
            nc.vector.scalar_tensor_tensor(res[h][:], p_ps[h][:], mean[h][:], minus[h][:], ALU.max, ALU.subtract)
            nc.sync.dma_start(out=out[h * HALF : (h + 1) * HALF, :], in_=res[h][:])

        quarters = ((0, HALF // 2), (HALF // 2, HALF))
        for i in range(2):
            for h in range(halves):
                pick("scalar", ga, list_a, h, i)
                pick("vector", gb, list_b, h, i)
        for h in range(halves):
            larger(h, 0)
        for i in range(2, 4):
            pick("scalar", ga, list_a, 0, i)
            pick("vector", gb, list_b, 0, i)
        for i in range(2, 4):
            pick("scalar", ga, list_a, 1, i)
        larger(0, 1)
        deal(nc.vector.tensor_copy, w2_codes[:].bitcast(I32), w2_raw[:].bitcast(I32))
        nc.sync.dma_start(out=wb_codes[:].bitcast(I32), in_=wb_words[0].bitcast(I32))
        for r in range(4):
            nc.sync.dma_start(out=wb_s[:].bitcast(I32)[r:P:32, :], in_=wb_scales[0, r:16:4, :].bitcast(I32))
        nc.sync.dma_start(out=resid[:], in_=rs.rearrange("(h p) n -> p h n", p=P))
        scale_round(0)
        deal(nc.scalar.copy, w_codes[:], w_raw[:])
        quantise(u_codes[0], u_s[0], u[0], E4M3)
        own_product(0)
        own_product(1)
        picked_product(0)
        for lo, hi in quarters:
            for i in range(2, 4):
                pick("scalar", gb, list_b, 1, i, lo, hi)
        for lo, hi in quarters:
            larger(1, 1, lo, hi)
        for lo, hi in quarters:
            scale_round(1, lo, hi)
        for lo, hi in quarters:
            quantise(u_codes[1], u_s[1], u[1], E4M3, lo, hi)
        picked_product(1)
        relu(0)
        lagged(0)
        quantise(hid_codes[0], hid_s[0], hid[0], E5M2)
        second_product(0)
        for lo, hi in quarters:
            relu(1, lo, hi)
        for lo, hi in quarters:
            lagged(1, lo, hi)
        for lo, hi in quarters:
            quantise(hid_codes[1], hid_s[1], hid[1], E5M2, lo, hi)
        second_product(1)
        finish(0)
        nc.scalar.activation(magn[1][:], p_ps[1][:], ACT.Abs, scale=1.0 / N, accum_out=mean[1][:])
        sides = (slice(0, N // 2), slice(N // 2, N))
        for side in sides:
            nc.vector.tensor_scalar(minus[1][:, side], resid[:, 1, side], 0.3, mean[1][:], ALU.mult, ALU.add)
        for side in sides:
            nc.vector.scalar_tensor_tensor(
                res[1][:, side], p_ps[1][:, side], mean[1][:], minus[1][:, side], ALU.max, ALU.subtract
            )
            nc.sync.dma_start(out=out[HALF:J, side], in_=res[1][:, side])
